import numpy as np
import ml_dtypes


def mxq(x, axis, fmt="e4m3"):
    dtype, down = {"e4m3": (ml_dtypes.float8_e4m3fn, 7), "e5m2": (ml_dtypes.float8_e5m2, 14)}[fmt]
    v = np.moveaxis(np.asarray(x, np.float32).astype(ml_dtypes.bfloat16).astype(np.float64), axis, -1)
    blocks = v.reshape(v.shape[:-1] + (-1, 32))
    amax = np.abs(blocks).max(-1, keepdims=True)
    byte = np.maximum(np.where(amax > 0, np.frexp(amax)[1] - 1 + 127, 0) - down, 1)
    scale = np.exp2(byte - 127.0)
    codes = (blocks / scale).astype(np.float32).astype(dtype).astype(np.float64)
    return np.moveaxis((codes * scale).reshape(v.shape), -1, axis)


WIDE = False


def mx_kscale(k):
    if not WIDE:
        return np.ones(k)
    levels = np.array([10, -10, 5, -5, 0])
    if k % 512:
        return np.exp2(np.random.permutation(np.resize(levels, k // 32))).repeat(32)
    a = np.empty((k // 512, 16))
    for p in range(k // 512):
        a[p, :8] = np.random.permutation(np.resize(levels, 8))
        for g in range(8):
            far = levels[np.abs(levels - a[p, g]) >= 10]
            a[p, g + 8] = far[np.random.randint(len(far))]
    return np.exp2(a.ravel()).repeat(32)


def f64(x):
    return np.asarray(x).astype(np.float64)


def striped(idx):
    return np.tile(idx.reshape(-1, 16).T, (8, 1)).astype(np.uint16)


def unstriped(offs):
    return offs[:16].T.reshape(-1).astype(np.int64)


K, T, E, C, N = 1024, 512, 8, 128, 128


def by_expert(wq, xq):
    return np.concatenate([wq[e].T @ xq[:, e * C:(e + 1) * C] for e in range(E)], axis=1)


def setup_inputs():
    n = np.random.standard_normal
    s = mx_kscale(K)[:, None]
    first = np.random.permutation(np.repeat(np.arange(E), T // E))
    second = (first + 1 + np.random.permutation(np.repeat(np.arange(E - 1), -(-T // (E - 1)))[:T])) % E
    while np.bincount(second, minlength=E).max() != T // E:
        load = np.bincount(second, minlength=E); hi, lo = int(load.argmax()), int(load.argmin())
        t = np.flatnonzero((second == hi) & (first != lo))[0]; second[t] = lo
    slot_token = np.empty(E * C, np.int64); pos = np.empty((2, T), np.int64); fill = np.zeros(E, np.int64)
    place = np.stack([np.random.permutation(C) for _ in range(E)])
    for r, deal in enumerate((first, second)):
        for t in np.random.permutation(T):
            e = deal[t]; j = e * C + place[e, fill[e]]; fill[e] += 1; slot_token[j] = t; pos[r, t] = j
    g = np.random.uniform(0.2, 0.8, T)
    return {
        "xT": (n((K, T)) * s).astype(np.float32),
        "w": (n((E, K, N)) / np.sqrt(K) / s[None]).astype(np.float32),
        "b": (0.3 * n((N, E))).astype(np.float32),
        "gate": np.stack([np.tile(g, (N, 1)), np.tile(1.0 - g, (N, 1))]).astype(np.float32),
        "offs": striped(slot_token),
        "pos1": striped(pos[0]),
        "pos2": striped(pos[1]),
    }


def reference(xT, w, b, gate, offs, pos1, pos2):
    idx = unstriped(offs)
    xq = mxq(f64(xT)[:, idx], 0, "e4m3")
    y = by_expert(mxq(f64(w), 1, "e4m3"), xq)
    y = y + np.repeat(f64(b), C, axis=1)
    return f64(gate[0]) * y[:, unstriped(pos1)] + f64(gate[1]) * y[:, unstriped(pos2)]

@@ -1,0 +1,123 @@
+from contextlib import ExitStack
+
+import concourse.mybir as mybir
+
+K, T, E, C, N = 1024, 512, 8, 128, 128
+FLOPS = 2 * K * E * C * N
+
+F32 = mybir.dt.float32
+BF16 = mybir.dt.bfloat16
+U32 = mybir.dt.uint32
+U16 = mybir.dt.uint16
+U8 = mybir.dt.uint8
+FP8X4 = mybir.dt.float8_e4m3fn_x4
+MULT = mybir.AluOpType.mult
+IDENTITY = mybir.ActivationFunctionType.Identity
+
+P = 128
+PACK = 4
+PASSES = K // (P * PACK)
+HALF = T // 2
+
+
+def tile_routed_moe_kernel(tc, xT, w, b, gate, offs, pos1, pos2, out):
+    nc = tc.nc
+    x_view = xT.rearrange("(a p j) t -> a p j t", p=P, j=PACK)
+    w_view = w.rearrange("e (a p j) n -> e p a (j n)", p=P, j=PACK)
+
+    with ExitStack() as ctx:
+        keep = ctx.enter_context(tc.tile_pool(name="keep", bufs=1))
+        psum = ctx.enter_context(tc.psum_pool(name="psum", bufs=1))
+
+        offs_t = keep.tile([P, E * C // 16], U16, name="offs_t")
+        pos1_t = keep.tile([P, T // 16], U16, name="pos1_t")
+        pos2_t = keep.tile([P, T // 16], U16, name="pos2_t")
+        bias = keep.tile([P, E], F32, name="bias")
+        gates = keep.tile([P, 2, T], F32, name="gates")
+
+        x_scales = keep.tile([P, T], U8, name="x_scales", align_bytes=64)
+        nc.gpsimd.memset(x_scales[:], 0)
+
+        x_raw = {}
+        for a in range(PASSES):
+            for h in range(2):
+                raw = keep.tile([P, PACK, HALF], F32, name=f"x_raw{a}{h}")
+                nc.sync.dma_start(out=raw[:], in_=x_view[a, :, :, h * HALF : (h + 1) * HALF])
+                x_raw[a, h] = raw
+        nc.sync.dma_start(offs_t[:], offs)
+        w_raw = []
+        for e in range(E):
+            raw = keep.tile([P, PASSES, PACK * N], F32, name=f"w_raw{e}")
+            nc.sync.dma_start(out=raw[:], in_=w_view[e])
+            w_raw.append(raw)
+        nc.sync.dma_start(pos1_t[:], pos1)
+        nc.sync.dma_start(pos2_t[:], pos2)
+        nc.sync.dma_start(bias[:], b)
+        nc.sync.dma_start(out=gates[:], in_=gate.rearrange("g p t -> p g t"))
+
+        g_words = []
+        g_scales = keep.tile([P, E * C], U8, name="g_scales", align_bytes=64)
+        cuts = [(0, 384), (384, 768), (768, 1024)]
+        for a in range(PASSES):
+            words = keep.tile([P, T], U32, name=f"x_words{a}", align_bytes=64)
+            for h in range(2):
+                grouped = keep.tile([P, HALF, PACK], BF16, name=f"x_grouped{a}{h}", align_bytes=64)
+                dst = grouped[:].rearrange("p (c i) t -> p c t i", i=4)
+                src = x_raw[a, h][:].rearrange("p t (c i) -> p c t i", i=4)
+                if a == 0:
+                    nc.vector.tensor_copy(out=dst, in_=src)
+                else:
+                    nc.scalar.copy(out=dst, in_=src)
+                nc.vector.quantize_mx(
+                    out=words[:, h * HALF : (h + 1) * HALF].bitcast(FP8X4),
+                    scales=x_scales[4 * a : P, h * HALF : (h + 1) * HALF],
+                    in_=grouped[:].rearrange("p w t -> p (w t)"),
+                )
+            gathered = keep.tile([P, E * C], U32, name=f"g_words{a}", align_bytes=64)
+            for lo, hi in cuts:
+                nc.vector.tensor_copy(out=gathered[:, lo:hi], in_=words[:].indirect(offs_t[:, lo // 16 : hi // 16]))
+            g_words.append(gathered)
+        for lo, hi in cuts:
+            nc.vector.tensor_copy(out=g_scales[:, lo:hi], in_=x_scales[:].indirect(offs_t[:, lo // 16 : hi // 16]))
+
+        y = keep.tile([P, E * C], F32, name="y")
+        for e in range(E):
+            grouped = keep.tile([P, PASSES, N, PACK], BF16, name=f"w_grouped{e}", align_bytes=64)
+            src = w_raw[e][:].rearrange("p a (t c i) -> p a c t i", t=PACK, i=4)
+            dst = grouped[:].rearrange("p a (c i) t -> p a c t i", i=4)
+            if e < E - 1:
+                nc.scalar.copy(out=dst, in_=src)
+            else:
+                nc.scalar.copy(out=dst[:, 0], in_=src[:, 0])
+                nc.vector.tensor_copy(out=dst[:, 1], in_=src[:, 1])
+            w_words = keep.tile([P, PASSES, N], U32, name=f"w_words{e}", align_bytes=64)
+            w_scales = keep.tile([P, PASSES, N], U8, name=f"w_scales{e}", align_bytes=64)
+            nc.vector.quantize_mx(
+                out=w_words[:].rearrange("p a n -> p (a n)").bitcast(FP8X4),
+                scales=w_scales[:].rearrange("p a n -> p (a n)"),
+                in_=grouped[:].rearrange("p a n t -> p (a n t)"),
+            )
+            slots = slice(e * C, (e + 1) * C)
+            acc = psum.tile([P, C], F32, name=f"acc{e}")
+            for a in range(PASSES):
+                nc.tensor.matmul_mx(
+                    out=acc[:],
+                    lhsT=w_words[:, a, :].bitcast(FP8X4),
+                    lhsT_scale=w_scales[:, a, :],
+                    rhs=g_words[a][:, slots].bitcast(FP8X4),
+                    rhs_scale=g_scales[4 * a : P, slots],
+                    start=(a == 0),
+                    stop=(a == PASSES - 1),
+                )
+            nc.scalar.activation(y[:, slots], acc[:], IDENTITY, bias=bias[:, e : e + 1])
+
+        for h in range(2):
+            cols = slice(h * HALF, (h + 1) * HALF)
+            list_cols = slice(h * HALF // 16, (h + 1) * HALF // 16)
+            part1 = keep.tile([P, HALF], F32, name=f"part1_{h}")
+            part2 = keep.tile([P, HALF], F32, name=f"part2_{h}")
+            total = keep.tile([P, HALF], F32, name=f"total{h}")
+            nc.vector.tensor_tensor(part1[:], y[:].indirect(pos1_t[:, list_cols]), gates[:, 0, cols], MULT)
+            nc.vector.tensor_tensor(part2[:], y[:].indirect(pos2_t[:, list_cols]), gates[:, 1, cols], MULT)
+            nc.vector.tensor_add(total[:], part1[:], part2[:])
+            nc.sync.dma_start(out=out[:, cols], in_=total[:])

@@ -8,6 +8,7 @@ FLOPS = 2 * K * E * C * N
 F32 = mybir.dt.float32
 BF16 = mybir.dt.bfloat16
 U32 = mybir.dt.uint32
+I32 = mybir.dt.int32
 U16 = mybir.dt.uint16
 U8 = mybir.dt.uint8
 FP8X4 = mybir.dt.float8_e4m3fn_x4
@@ -18,12 +19,24 @@ P = 128
 PACK = 4
 PASSES = K // (P * PACK)
 HALF = T // 2
+WINDOW = 1376
+X_SPLIT = (64, 64, 256, 256)
+LOADS = tuple((2 * e, 2) for e in range(E - 1)) + ((14, 1), (15, 1))
+GROUPS = ((0, 2), (2, 2), (4, 2), (6, 1), (7, 1))
+GPSIMD_EXPERTS = (1,)
+CUT = 384
 
 
 def tile_routed_moe_kernel(tc, xT, w, b, gate, offs, pos1, pos2, out):
     nc = tc.nc
     x_view = xT.rearrange("(a p j) t -> a p j t", p=P, j=PACK)
-    w_view = w.rearrange("e (a p j) n -> e p a (j n)", p=P, j=PACK)
+    w_view = w.rearrange("e (a p j) n -> p (e a) (j n)", p=P, j=PACK)
+
+    def interleave(copy, dst, src):
+        if len(src.shape) == 3:
+            copy(out=dst.rearrange("p (c i) t -> p c t i", i=4), in_=src.rearrange("p t (c i) -> p c t i", i=4))
+        else:
+            copy(out=dst.rearrange("p a (c i) t -> p a c t i", i=4), in_=src.rearrange("p a t (c i) -> p a c t i", i=4))
 
     with ExitStack() as ctx:
         keep = ctx.enter_context(tc.tile_pool(name="keep", bufs=1))
@@ -35,89 +48,98 @@ def tile_routed_moe_kernel(tc, xT, w, b, gate, offs, pos1, pos2, out):
         bias = keep.tile([P, E], F32, name="bias")
         gates = keep.tile([P, 2, T], F32, name="gates")
 
-        x_scales = keep.tile([P, T], U8, name="x_scales", align_bytes=64)
+        x_scales = keep.tile([P, WINDOW], U8, name="x_scales", align_bytes=64)
         nc.gpsimd.memset(x_scales[:], 0)
-
-        x_raw = {}
+        x_words = []
         for a in range(PASSES):
-            for h in range(2):
-                raw = keep.tile([P, PACK, HALF], F32, name=f"x_raw{a}{h}")
-                nc.sync.dma_start(out=raw[:], in_=x_view[a, :, :, h * HALF : (h + 1) * HALF])
-                x_raw[a, h] = raw
+            words = keep.tile([P, WINDOW], I32, name=f"x_words{a}", align_bytes=64)
+            nc.vector.memset(words[:, T:WINDOW], 0)
+            x_words.append(words)
+
         nc.sync.dma_start(offs_t[:], offs)
+        x_raw = {}
+        for a, h, width in ((0, 0, 1), (0, 1, 1), (1, 0, 1), (1, 1, 1)):
+            raw = keep.tile([P, PACK, width * HALF], F32, name=f"x_raw{a}{h}")
+            nc.sync.dma_start(out=raw[:], in_=x_view[a, :, :, h * HALF : (h + width) * HALF])
+            for i in range(width):
+                x_raw[a, h + i] = raw[:, :, i * HALF : (i + 1) * HALF]
         w_raw = []
-        for e in range(E):
-            raw = keep.tile([P, PASSES, PACK * N], F32, name=f"w_raw{e}")
-            nc.sync.dma_start(out=raw[:], in_=w_view[e])
-            w_raw.append(raw)
+        for first, count in LOADS:
+            raw = keep.tile([P, count, PACK, N], F32, name=f"w_raw{first}")
+            nc.sync.dma_start(out=raw[:].rearrange("p s j n -> p s (j n)"), in_=w_view[:, first : first + count])
+            for i in range(0, count, PASSES):
+                w_raw.append(raw[:, i : i + PASSES] if count > 1 else raw)
+        nc.sync.dma_start(bias[:], b)
         nc.sync.dma_start(pos1_t[:], pos1)
         nc.sync.dma_start(pos2_t[:], pos2)
-        nc.sync.dma_start(bias[:], b)
         nc.sync.dma_start(out=gates[:], in_=gate.rearrange("g p t -> p g t"))
 
         g_words = []
-        g_scales = keep.tile([P, E * C], U8, name="g_scales", align_bytes=64)
-        cuts = [(0, 384), (384, 768), (768, 1024)]
         for a in range(PASSES):
-            words = keep.tile([P, T], U32, name=f"x_words{a}", align_bytes=64)
             for h in range(2):
+                cols = slice(h * HALF, (h + 1) * HALF)
                 grouped = keep.tile([P, HALF, PACK], BF16, name=f"x_grouped{a}{h}", align_bytes=64)
-                dst = grouped[:].rearrange("p (c i) t -> p c t i", i=4)
-                src = x_raw[a, h][:].rearrange("p t (c i) -> p c t i", i=4)
-                if a == 0:
-                    nc.vector.tensor_copy(out=dst, in_=src)
-                else:
-                    nc.scalar.copy(out=dst, in_=src)
+                split = X_SPLIT[2 * a + h]
+                if split > 0:
+                    interleave(nc.scalar.copy, grouped[:, 0:split], x_raw[a, h][:, :, 0:split])
+                if split < HALF:
+                    interleave(nc.vector.tensor_copy, grouped[:, split:HALF], x_raw[a, h][:, :, split:HALF])
                 nc.vector.quantize_mx(
-                    out=words[:, h * HALF : (h + 1) * HALF].bitcast(FP8X4),
-                    scales=x_scales[4 * a : P, h * HALF : (h + 1) * HALF],
+                    out=x_words[a][:, cols].bitcast(FP8X4),
+                    scales=x_scales[4 * a : P, cols],
                     in_=grouped[:].rearrange("p w t -> p (w t)"),
                 )
             gathered = keep.tile([P, E * C], U32, name=f"g_words{a}", align_bytes=64)
-            for lo, hi in cuts:
-                nc.vector.tensor_copy(out=gathered[:, lo:hi], in_=words[:].indirect(offs_t[:, lo // 16 : hi // 16]))
+            nc.vector.tensor_copy(out=gathered[:], in_=x_words[a][:].bitcast(U32).indirect(offs_t[:]))
             g_words.append(gathered)
-        for lo, hi in cuts:
+        g_scales = keep.tile([P, E * C], U8, name="g_scales", align_bytes=64)
+        for lo, hi in ((0, 512), (512, 1024)):
             nc.vector.tensor_copy(out=g_scales[:, lo:hi], in_=x_scales[:].indirect(offs_t[:, lo // 16 : hi // 16]))
 
         y = keep.tile([P, E * C], F32, name="y")
-        for e in range(E):
-            grouped = keep.tile([P, PASSES, N, PACK], BF16, name=f"w_grouped{e}", align_bytes=64)
-            src = w_raw[e][:].rearrange("p a (t c i) -> p a c t i", t=PACK, i=4)
-            dst = grouped[:].rearrange("p a (c i) t -> p a c t i", i=4)
-            if e < E - 1:
-                nc.scalar.copy(out=dst, in_=src)
-            else:
-                nc.scalar.copy(out=dst[:, 0], in_=src[:, 0])
-                nc.vector.tensor_copy(out=dst[:, 1], in_=src[:, 1])
-            w_words = keep.tile([P, PASSES, N], U32, name=f"w_words{e}", align_bytes=64)
-            w_scales = keep.tile([P, PASSES, N], U8, name=f"w_scales{e}", align_bytes=64)
-            nc.vector.quantize_mx(
-                out=w_words[:].rearrange("p a n -> p (a n)").bitcast(FP8X4),
-                scales=w_scales[:].rearrange("p a n -> p (a n)"),
-                in_=grouped[:].rearrange("p a n t -> p (a n t)"),
-            )
-            slots = slice(e * C, (e + 1) * C)
-            acc = psum.tile([P, C], F32, name=f"acc{e}")
-            for a in range(PASSES):
-                nc.tensor.matmul_mx(
-                    out=acc[:],
-                    lhsT=w_words[:, a, :].bitcast(FP8X4),
-                    lhsT_scale=w_scales[:, a, :],
-                    rhs=g_words[a][:, slots].bitcast(FP8X4),
-                    rhs_scale=g_scales[4 * a : P, slots],
-                    start=(a == 0),
-                    stop=(a == PASSES - 1),
+        for first, count in GROUPS:
+            grouped = keep.tile([P, count, PASSES, N, PACK], BF16, name=f"w_grouped{first}", align_bytes=64)
+            words = keep.tile([P, count, PASSES, N], U32, name=f"w_words{first}", align_bytes=64)
+            scales = keep.tile([P, count, PASSES, N], U8, name=f"w_scales{first}", align_bytes=64)
+            for i in range(count):
+                e = first + i
+                if e == E - 1:
+                    interleave(nc.scalar.copy, grouped[:, i, 0], w_raw[e][:, 0])
+                    interleave(nc.vector.tensor_copy, grouped[:, i, 1], w_raw[e + 1][:, 0])
+                elif e in GPSIMD_EXPERTS:
+                    interleave(nc.gpsimd.tensor_copy, grouped[:, i], w_raw[e][:])
+                else:
+                    interleave(nc.scalar.copy, grouped[:, i], w_raw[e][:])
+            pieces = PASSES if first == E - 1 else 1
+            width = count * PASSES * N // pieces
+            for q in range(pieces):
+                cols = slice(q * width, (q + 1) * width)
+                nc.vector.quantize_mx(
+                    out=words[:].rearrange("p e a n -> p (e a n)")[:, cols].bitcast(FP8X4),
+                    scales=scales[:].rearrange("p e a n -> p (e a n)")[:, cols],
+                    in_=grouped[:].rearrange("p e a n t -> p (e a n t)")[:, q * width * PACK : (q + 1) * width * PACK],
                 )
-            nc.scalar.activation(y[:, slots], acc[:], IDENTITY, bias=bias[:, e : e + 1])
+            for i in range(count):
+                e = first + i
+                slots = slice(e * C, (e + 1) * C)
+                acc = psum.tile([P, C], F32, name=f"acc{e}")
+                for a in range(PASSES):
+                    nc.tensor.matmul_mx(
+                        out=acc[:],
+                        lhsT=words[:, i, a, :].bitcast(FP8X4),
+                        lhsT_scale=scales[:, i, a, :],
+                        rhs=g_words[a][:, slots].bitcast(FP8X4),
+                        rhs_scale=g_scales[4 * a : P, slots],
+                        start=(a == 0),
+                        stop=(a == PASSES - 1),
+                    )
+                nc.scalar.activation(y[:, slots], acc[:], IDENTITY, bias=bias[:, e : e + 1])
 
-        for h in range(2):
-            cols = slice(h * HALF, (h + 1) * HALF)
-            list_cols = slice(h * HALF // 16, (h + 1) * HALF // 16)
-            part1 = keep.tile([P, HALF], F32, name=f"part1_{h}")
-            part2 = keep.tile([P, HALF], F32, name=f"part2_{h}")
-            total = keep.tile([P, HALF], F32, name=f"total{h}")
-            nc.vector.tensor_tensor(part1[:], y[:].indirect(pos1_t[:, list_cols]), gates[:, 0, cols], MULT)
-            nc.vector.tensor_tensor(part2[:], y[:].indirect(pos2_t[:, list_cols]), gates[:, 1, cols], MULT)
-            nc.vector.tensor_add(total[:], part1[:], part2[:])
-            nc.sync.dma_start(out=out[:, cols], in_=total[:])
+        part1 = keep.tile([P, T], F32, name="part1")
+        nc.vector.tensor_tensor(part1[:], y[:].indirect(pos1_t[:]), gates[:, 0, :], MULT)
+        for lo, hi in ((0, CUT), (CUT, T)):
+            part2 = keep.tile([P, hi - lo], F32, name=f"part2_{lo}")
+            total = keep.tile([P, hi - lo], F32, name=f"total{lo}")
+            nc.vector.tensor_tensor(part2[:], y[:].indirect(pos2_t[:, lo // 16 : hi // 16]), gates[:, 1, lo:hi], MULT)
+            nc.vector.tensor_add(total[:], part1[:, lo:hi], part2[:])
+            nc.sync.dma_start(out=out[:, lo:hi], in_=total[:])

@@ -23,8 +23,8 @@ WINDOW = 1376
 X_SPLIT = (64, 64, 256, 256)
 LOADS = tuple((2 * e, 2) for e in range(E - 1)) + ((14, 1), (15, 1))
 GROUPS = ((0, 2), (2, 2), (4, 2), (6, 1), (7, 1))
-GPSIMD_EXPERTS = (1,)
-CUT = 384
+VECTOR_EXPERTS = (2,)
+CUT = 320
 
 
 def tile_routed_moe_kernel(tc, xT, w, b, gate, offs, pos1, pos2, out):
@@ -106,8 +106,8 @@ def tile_routed_moe_kernel(tc, xT, w, b, gate, offs, pos1, pos2, out):
                 if e == E - 1:
                     interleave(nc.scalar.copy, grouped[:, i, 0], w_raw[e][:, 0])
                     interleave(nc.vector.tensor_copy, grouped[:, i, 1], w_raw[e + 1][:, 0])
-                elif e in GPSIMD_EXPERTS:
-                    interleave(nc.gpsimd.tensor_copy, grouped[:, i], w_raw[e][:])
+                elif e in VECTOR_EXPERTS:
+                    interleave(nc.vector.tensor_copy, grouped[:, i], w_raw[e][:])
                 else:
                     interleave(nc.scalar.copy, grouped[:, i], w_raw[e][:])
             pieces = PASSES if first == E - 1 else 1
@@ -137,9 +137,13 @@ def tile_routed_moe_kernel(tc, xT, w, b, gate, offs, pos1, pos2, out):
 
         part1 = keep.tile([P, T], F32, name="part1")
         nc.vector.tensor_tensor(part1[:], y[:].indirect(pos1_t[:]), gates[:, 0, :], MULT)
-        for lo, hi in ((0, CUT), (CUT, T)):
-            part2 = keep.tile([P, hi - lo], F32, name=f"part2_{lo}")
+        pieces = ((0, CUT), (CUT, T))
+        part2 = []
+        for lo, hi in pieces:
+            part = keep.tile([P, hi - lo], F32, name=f"part2_{lo}")
+            nc.vector.tensor_tensor(part[:], y[:].indirect(pos2_t[:, lo // 16 : hi // 16]), gates[:, 1, lo:hi], MULT)
+            part2.append(part)
+        for (lo, hi), part in zip(pieces, part2):
             total = keep.tile([P, hi - lo], F32, name=f"total{lo}")
-            nc.vector.tensor_tensor(part2[:], y[:].indirect(pos2_t[:, lo // 16 : hi // 16]), gates[:, 1, lo:hi], MULT)
-            nc.vector.tensor_add(total[:], part1[:, lo:hi], part2[:])
+            nc.vector.tensor_add(total[:], part1[:, lo:hi], part[:])
             nc.sync.dma_start(out=out[:, lo:hi], in_=total[:])

@@ -20,10 +20,10 @@ PACK = 4
 PASSES = K // (P * PACK)
 HALF = T // 2
 WINDOW = 1376
-X_SPLIT = (64, 64, 256, 256)
+X_SPLIT = (64, 112, 256, 256)
 LOADS = tuple((2 * e, 2) for e in range(E - 1)) + ((14, 1), (15, 1))
 GROUPS = ((0, 2), (2, 2), (4, 2), (6, 1), (7, 1))
-VECTOR_EXPERTS = (2,)
+VECTOR_EXPERTS = (4, 6)
 CUT = 320
 
 
@@ -56,13 +56,13 @@ def tile_routed_moe_kernel(tc, xT, w, b, gate, offs, pos1, pos2, out):
             nc.vector.memset(words[:, T:WINDOW], 0)
             x_words.append(words)
 
-        nc.sync.dma_start(offs_t[:], offs)
         x_raw = {}
         for a, h, width in ((0, 0, 1), (0, 1, 1), (1, 0, 1), (1, 1, 1)):
             raw = keep.tile([P, PACK, width * HALF], F32, name=f"x_raw{a}{h}")
             nc.sync.dma_start(out=raw[:], in_=x_view[a, :, :, h * HALF : (h + width) * HALF])
-            for i in range(width):
-                x_raw[a, h + i] = raw[:, :, i * HALF : (i + 1) * HALF]
+            x_raw[a, h] = raw
+            if (a, h) == (0, 1):
+                nc.sync.dma_start(offs_t[:], offs)
         w_raw = []
         for first, count in LOADS:
             raw = keep.tile([P, count, PACK, N], F32, name=f"w_raw{first}")

from contextlib import ExitStack

import concourse.mybir as mybir

K, T, E, C, N = 1024, 512, 8, 128, 128
FLOPS = 2 * K * E * C * N

F32 = mybir.dt.float32
BF16 = mybir.dt.bfloat16
U32 = mybir.dt.uint32
I32 = mybir.dt.int32
U16 = mybir.dt.uint16
U8 = mybir.dt.uint8
FP8X4 = mybir.dt.float8_e4m3fn_x4
MULT = mybir.AluOpType.mult
IDENTITY = mybir.ActivationFunctionType.Identity

P = 128
PACK = 4
PASSES = K // (P * PACK)
HALF = T // 2
WINDOW = 1376
X_SPLIT = (64, 112, 256, 256)
LOADS = tuple((2 * e, 2) for e in range(E - 1)) + ((14, 1), (15, 1))
GROUPS = ((0, 2), (2, 2), (4, 2), (6, 1), (7, 1))
VECTOR_EXPERTS = (4, 6)
CUT = 320


def tile_routed_moe_kernel(tc, xT, w, b, gate, offs, pos1, pos2, out):
    nc = tc.nc
    x_view = xT.rearrange("(a p j) t -> a p j t", p=P, j=PACK)
    w_view = w.rearrange("e (a p j) n -> p (e a) (j n)", p=P, j=PACK)

    def interleave(copy, dst, src):
        if len(src.shape) == 3:
            copy(out=dst.rearrange("p (c i) t -> p c t i", i=4), in_=src.rearrange("p t (c i) -> p c t i", i=4))
        else:
            copy(out=dst.rearrange("p a (c i) t -> p a c t i", i=4), in_=src.rearrange("p a t (c i) -> p a c t i", i=4))

    with ExitStack() as ctx:
        keep = ctx.enter_context(tc.tile_pool(name="keep", bufs=1))
        psum = ctx.enter_context(tc.psum_pool(name="psum", bufs=1))

        offs_t = keep.tile([P, E * C // 16], U16, name="offs_t")
        pos1_t = keep.tile([P, T // 16], U16, name="pos1_t")
        pos2_t = keep.tile([P, T // 16], U16, name="pos2_t")
        bias = keep.tile([P, E], F32, name="bias")
        gates = keep.tile([P, 2, T], F32, name="gates")

        x_scales = keep.tile([P, WINDOW], U8, name="x_scales", align_bytes=64)
        nc.gpsimd.memset(x_scales[:], 0)
        x_words = []
        for a in range(PASSES):
            words = keep.tile([P, WINDOW], I32, name=f"x_words{a}", align_bytes=64)
            nc.vector.memset(words[:, T:WINDOW], 0)
            x_words.append(words)

        x_raw = {}
        for a, h, width in ((0, 0, 1), (0, 1, 1), (1, 0, 1), (1, 1, 1)):
            raw = keep.tile([P, PACK, width * HALF], F32, name=f"x_raw{a}{h}")
            nc.sync.dma_start(out=raw[:], in_=x_view[a, :, :, h * HALF : (h + width) * HALF])
            x_raw[a, h] = raw
            if (a, h) == (0, 1):
                nc.sync.dma_start(offs_t[:], offs)
        w_raw = []
        for first, count in LOADS:
            raw = keep.tile([P, count, PACK, N], F32, name=f"w_raw{first}")
            nc.sync.dma_start(out=raw[:].rearrange("p s j n -> p s (j n)"), in_=w_view[:, first : first + count])
            for i in range(0, count, PASSES):
                w_raw.append(raw[:, i : i + PASSES] if count > 1 else raw)
        nc.sync.dma_start(bias[:], b)
        nc.sync.dma_start(pos1_t[:], pos1)
        nc.sync.dma_start(pos2_t[:], pos2)
        nc.sync.dma_start(out=gates[:], in_=gate.rearrange("g p t -> p g t"))

        g_words = []
        for a in range(PASSES):
            for h in range(2):
                cols = slice(h * HALF, (h + 1) * HALF)
                grouped = keep.tile([P, HALF, PACK], BF16, name=f"x_grouped{a}{h}", align_bytes=64)
                split = X_SPLIT[2 * a + h]
                if split > 0:
                    interleave(nc.scalar.copy, grouped[:, 0:split], x_raw[a, h][:, :, 0:split])
                if split < HALF:
                    interleave(nc.vector.tensor_copy, grouped[:, split:HALF], x_raw[a, h][:, :, split:HALF])
                nc.vector.quantize_mx(
                    out=x_words[a][:, cols].bitcast(FP8X4),
                    scales=x_scales[4 * a : P, cols],
                    in_=grouped[:].rearrange("p w t -> p (w t)"),
                )
            gathered = keep.tile([P, E * C], U32, name=f"g_words{a}", align_bytes=64)
            nc.vector.tensor_copy(out=gathered[:], in_=x_words[a][:].bitcast(U32).indirect(offs_t[:]))
            g_words.append(gathered)
        g_scales = keep.tile([P, E * C], U8, name="g_scales", align_bytes=64)
        for lo, hi in ((0, 512), (512, 1024)):
            nc.vector.tensor_copy(out=g_scales[:, lo:hi], in_=x_scales[:].indirect(offs_t[:, lo // 16 : hi // 16]))

        y = keep.tile([P, E * C], F32, name="y")
        for first, count in GROUPS:
            grouped = keep.tile([P, count, PASSES, N, PACK], BF16, name=f"w_grouped{first}", align_bytes=64)
            words = keep.tile([P, count, PASSES, N], U32, name=f"w_words{first}", align_bytes=64)
            scales = keep.tile([P, count, PASSES, N], U8, name=f"w_scales{first}", align_bytes=64)
            for i in range(count):
                e = first + i
                if e == E - 1:
                    interleave(nc.scalar.copy, grouped[:, i, 0], w_raw[e][:, 0])
                    interleave(nc.vector.tensor_copy, grouped[:, i, 1], w_raw[e + 1][:, 0])
                elif e in VECTOR_EXPERTS:
                    interleave(nc.vector.tensor_copy, grouped[:, i], w_raw[e][:])
                else:
                    interleave(nc.scalar.copy, grouped[:, i], w_raw[e][:])
            pieces = PASSES if first == E - 1 else 1
            width = count * PASSES * N // pieces
            for q in range(pieces):
                cols = slice(q * width, (q + 1) * width)
                nc.vector.quantize_mx(
                    out=words[:].rearrange("p e a n -> p (e a n)")[:, cols].bitcast(FP8X4),
                    scales=scales[:].rearrange("p e a n -> p (e a n)")[:, cols],
                    in_=grouped[:].rearrange("p e a n t -> p (e a n t)")[:, q * width * PACK : (q + 1) * width * PACK],
                )
            for i in range(count):
                e = first + i
                slots = slice(e * C, (e + 1) * C)
                acc = psum.tile([P, C], F32, name=f"acc{e}")
                for a in range(PASSES):
                    nc.tensor.matmul_mx(
                        out=acc[:],
                        lhsT=words[:, i, a, :].bitcast(FP8X4),
                        lhsT_scale=scales[:, i, a, :],
                        rhs=g_words[a][:, slots].bitcast(FP8X4),
                        rhs_scale=g_scales[4 * a : P, slots],
                        start=(a == 0),
                        stop=(a == PASSES - 1),
                    )
                nc.scalar.activation(y[:, slots], acc[:], IDENTITY, bias=bias[:, e : e + 1])

        part1 = keep.tile([P, T], F32, name="part1")
        nc.vector.tensor_tensor(part1[:], y[:].indirect(pos1_t[:]), gates[:, 0, :], MULT)
        pieces = ((0, CUT), (CUT, T))
        part2 = []
        for lo, hi in pieces:
            part = keep.tile([P, hi - lo], F32, name=f"part2_{lo}")
            nc.vector.tensor_tensor(part[:], y[:].indirect(pos2_t[:, lo // 16 : hi // 16]), gates[:, 1, lo:hi], MULT)
            part2.append(part)
        for (lo, hi), part in zip(pieces, part2):
            total = keep.tile([P, hi - lo], F32, name=f"total{lo}")
            nc.vector.tensor_add(total[:], part1[:, lo:hi], part[:])
            nc.sync.dma_start(out=out[:, lo:hi], in_=total[:])
